import numpy as np
import ml_dtypes


def mxq(x, axis, fmt="e4m3"):
    dtype, down = {"e4m3": (ml_dtypes.float8_e4m3fn, 7), "e5m2": (ml_dtypes.float8_e5m2, 14)}[fmt]
    v = np.moveaxis(np.asarray(x, np.float32).astype(ml_dtypes.bfloat16).astype(np.float64), axis, -1)
    blocks = v.reshape(v.shape[:-1] + (-1, 32))
    amax = np.abs(blocks).max(-1, keepdims=True)
    byte = np.maximum(np.where(amax > 0, np.frexp(amax)[1] - 1 + 127, 0) - down, 1)
    scale = np.exp2(byte - 127.0)
    codes = (blocks / scale).astype(np.float32).astype(dtype).astype(np.float64)
    return np.moveaxis((codes * scale).reshape(v.shape), -1, axis)


WIDE = False


def mx_kscale(k):
    if not WIDE:
        return np.ones(k)
    levels = np.array([10, -10, 5, -5, 0])
    if k % 512:
        return np.exp2(np.random.permutation(np.resize(levels, k // 32))).repeat(32)
    a = np.empty((k // 512, 16))
    for p in range(k // 512):
        a[p, :8] = np.random.permutation(np.resize(levels, 8))
        for g in range(8):
            far = levels[np.abs(levels - a[p, g]) >= 10]
            a[p, g + 8] = far[np.random.randint(len(far))]
    return np.exp2(a.ravel()).repeat(32)


def f64(x):
    return np.asarray(x).astype(np.float64)


def striped8(idx):
    return np.asarray(idx).reshape(8, -1, 16).transpose(0, 2, 1).reshape(128, -1).astype(np.uint16)


def unstriped8(offs):
    return offs.reshape(8, 16, -1).transpose(0, 2, 1).reshape(8, -1).astype(np.int64)


def pick8(x, idx, run):
    r = np.arange(len(x))
    return x[r[:, None], idx[r % (8 * run) // run]]


E2M1 = np.array([0.0, 0.5, 1.0, 1.5, 2.0, 3.0, 4.0, 6.0, -0.0, -0.5, -1.0, -1.5, -2.0, -3.0, -4.0, -6.0])


def pack_weight(w, fmt):
    k, n = w.shape
    w = f64(np.asarray(w, np.float32).astype(ml_dtypes.bfloat16)).reshape(k // 32, 32, n)
    amax = np.abs(w).max(1)
    if fmt == "e4m3":
        byte = np.frexp(amax)[1] - 1 + 127 - 7
    else:
        mant, ex = np.frexp(amax / 6.0)
        byte = np.where(mant > 0.5, ex, ex - 1) + 127
    byte = np.clip(np.where(amax > 0, byte, 1), 1, 254)
    scaled = (w * np.exp2(127.0 - byte)[:, None, :]).reshape(k, n).astype(np.float32)
    by_word = np.ascontiguousarray(scaled.reshape(k // 512, 128, 4, n).transpose(0, 1, 3, 2))
    if fmt == "e4m3":
        words = by_word.astype(ml_dtypes.float8_e4m3fn).view(np.uint8)
    else:
        c = by_word.astype(ml_dtypes.float4_e2m1fn).view(np.uint8) & 0xF
        words = (c[..., 0::2] | (c[..., 1::2] << 4)).reshape(k // 512, 128, 2 * n)
    return np.ascontiguousarray(words), np.ascontiguousarray(byte.astype(np.uint8).reshape(k // 512, 16, n))


def unpack_weight(words, scales, fmt):
    g, _, n = scales.shape
    words = np.ascontiguousarray(words).reshape(g, 128, n, -1)
    if fmt == "e4m3":
        vals = words.view(ml_dtypes.float8_e4m3fn).astype(np.float64)
    else:
        nib = np.empty((g, 128, n, 4), np.uint8)
        nib[..., 0::2] = words & 0xF
        nib[..., 1::2] = words >> 4
        vals = E2M1[nib]
    vals = vals * np.repeat(np.exp2(scales.astype(np.float64) - 127.0), 8, axis=1)[..., None]
    return vals.transpose(0, 1, 3, 2).reshape(g * 512, n)


D, T, I, Q = 512, 1024, 512, 128


def setup_inputs():
    n = np.random.standard_normal
    idx = np.stack([np.random.permutation(T)[:I] for _ in range(8)])
    idx2 = np.stack([np.random.permutation(T)[:I] for _ in range(8)])
    idx3 = np.stack([np.random.permutation(T)[:I] for _ in range(8)])
    idx4 = np.stack([np.random.permutation(T)[:I] for _ in range(8)])
    fd = mx_kscale(D)
    keysp = pack_weight(n((D, T)) / fd[:, None], "e4m3")
    return {
        "query": (n((D, Q)) * 1.0 / np.sqrt(D) * fd[:, None]).astype(np.float32),
        "keys_words": keysp[0],
        "keys_scales": keysp[1],
        "lam": (np.random.uniform(0.4, 1.0, (Q, 1))).astype(np.float32),
        "old": (1.0 * n((Q, T))).astype(np.float32),
        "share2": (np.random.uniform(0.4, 1.2, (Q, 1))).astype(np.float32),
        "offs": striped8(idx),
        "offs2": striped8(idx2),
        "offs3": striped8(idx3),
        "offs4": striped8(idx4),
    }


def reference(query, keys_words, keys_scales, lam, old, share2, offs, offs2, offs3, offs4):
    idx = unstriped8(offs)
    idx2 = unstriped8(offs2)
    idx3 = unstriped8(offs3)
    idx4 = unstriped8(offs4)
    keysu = unpack_weight(keys_words, keys_scales, "e4m3")
    queryq = mxq(f64(query), 0, "e4m3")
    a = queryq.T @ keysu
    w = pick8(a, idx, 16) + np.tanh(pick8(a, idx2, 16) - pick8(a, idx3, 16)) * f64(lam)
    f1 = np.zeros((Q, T))
    f1[np.arange(Q)[:, None], idx[np.arange(Q) % 128 // 16]] = w
    f2 = np.zeros((Q, T))
    f2[np.arange(Q)[:, None], idx4[np.arange(Q) % 128 // 16]] = w
    y = f64(old) + f1 + f2 * f64(share2)
    return y

@@ -1,0 +1,159 @@
+from contextlib import ExitStack
+
+import concourse.mybir as mybir
+from concourse.masks import make_identity
+
+D, T, SLOTS, Q = 512, 1024, 512, 128
+FLOPS = 2 * D * Q * T
+
+F32 = mybir.dt.float32
+BF16 = mybir.dt.bfloat16
+I32 = mybir.dt.int32
+U32 = mybir.dt.uint32
+U16 = mybir.dt.uint16
+U8 = mybir.dt.uint8
+FP8X4 = mybir.dt.float8_e4m3fn_x4
+ALU = mybir.AluOpType
+ACT = mybir.ActivationFunctionType
+
+P = 128
+PACK = 4
+N_MM = 256
+HALF = SLOTS // 2
+LIST_COLS = SLOTS // 16
+BANK = 512
+PIECE = 256
+
+
+def tile_attend_seconded_lean_twiceput_heads_kernel(
+    tc, query, keys_words, keys_scales, lam, old, share2, offs, offs2, offs3, offs4, out
+):
+    nc = tc.nc
+    with ExitStack() as ctx:
+        sb = ctx.enter_context(tc.tile_pool(name="sb", bufs=1))
+        ps = ctx.enter_context(tc.psum_pool(name="ps", bufs=1))
+
+        k_scales = sb.tile([P, T], U8, name="k_scales", align_bytes=64)
+        nc.vector.memset(k_scales[:].bitcast(I32), 0)
+
+        q_raw = sb.tile([P, PACK, Q], F32, name="q_raw")
+        nc.sync.dma_start(out=q_raw[:], in_=query.rearrange("(p j) q -> p j q", j=PACK))
+        for quad in range(4):
+            nc.sync.dma_start(
+                out=k_scales[32 * quad : 32 * quad + 4, :].bitcast(I32),
+                in_=keys_scales[0, 4 * quad : 4 * quad + 4, :].bitcast(I32),
+            )
+        words_hbm = keys_words[0].rearrange("p n t -> p (n t)").bitcast(I32)
+        k_words = []
+        for h in range(2):
+            tile = sb.tile([P, BANK], U32, name="k_words%d" % h, align_bytes=64)
+            nc.sync.dma_start(out=tile[:].bitcast(I32), in_=words_hbm[:, h * BANK : (h + 1) * BANK])
+            k_words.append(tile)
+
+        def load_list(src, name):
+            tile = sb.tile([P, LIST_COLS], U16, name=name)
+            nc.sync.dma_start(tile[:], src)
+            return tile
+
+        l_opp = load_list(offs3, "l_opp")
+        l_own = load_list(offs, "l_own")
+        l_sec = load_list(offs2, "l_sec")
+        lam_sb = sb.tile([P, 1], F32, name="lam_sb")
+        nc.sync.dma_start(out=lam_sb[:], in_=lam)
+        l_put = load_list(offs4, "l_put")
+        old_sb = sb.tile([P, T], F32, name="old_sb")
+        nc.sync.dma_start(out=old_sb[:], in_=old)
+        share_sb = sb.tile([P, 1], F32, name="share_sb")
+        nc.sync.dma_start(out=share_sb[:], in_=share2)
+
+        f1 = sb.tile([P, T], F32, name="f1")
+        f2 = sb.tile([P, T], F32, name="f2")
+        nc.vector.memset(f1[:], 0.0)
+        nc.vector.memset(f2[:], 0.0)
+        ident = sb.tile([P, P], F32, name="ident")
+        make_identity(nc, ident[:])
+
+        q_bf = sb.tile([P, Q, PACK], BF16, name="q_bf", align_bytes=64)
+        nc.vector.tensor_copy(
+            out=q_bf[:].rearrange("p (c i) t -> p c t i", i=4),
+            in_=q_raw[:].rearrange("p t (c i) -> p c t i", i=4),
+        )
+        q_codes = sb.tile([P, Q], U32, name="q_codes", align_bytes=64)
+        q_scales = sb.tile([P, Q], U8, name="q_scales", align_bytes=64)
+        nc.vector.quantize_mx(
+            out=q_codes[:].bitcast(FP8X4), scales=q_scales[:], in_=q_bf[:].rearrange("p q t -> p (q t)")
+        )
+
+        a = sb.tile([P, T], F32, name="a")
+        for c in range(T // N_MM):
+            cols = slice(c * N_MM, (c + 1) * N_MM)
+            bank = ps.tile([P, BANK], F32, name="scores%d" % c, tag="bank%d" % c)
+            lo = (c * N_MM) % BANK
+            nc.tensor.matmul_mx(
+                out=bank[:, 0:N_MM],
+                lhsT=q_codes[:].bitcast(FP8X4),
+                lhsT_scale=q_scales[:],
+                rhs=k_words[c * N_MM // BANK][:, lo : lo + N_MM].bitcast(FP8X4),
+                rhs_scale=k_scales[:, cols],
+                start=True,
+                stop=True,
+            )
+            if c % 2 == 0:
+                nc.scalar.activation(a[:, cols], bank[:, 0:N_MM], ACT.Copy)
+            else:
+                nc.vector.tensor_copy(out=a[:, cols], in_=bank[:, 0:N_MM])
+
+        n_pieces = T // PIECE
+        sum_t = [ps.tile([P, BANK], F32, name="sum_t%d" % b, tag="bank%d" % b) for b in range(n_pieces)]
+        for blk in range(T // P):
+            b, lo = divmod(blk * P, PIECE)
+            nc.tensor.matmul(
+                sum_t[b][:, lo : lo + P], old_sb[:, blk * P : (blk + 1) * P], ident[:],
+                start=(lo == 0), stop=False, is_transpose=True,
+            )
+
+        work = sb.tile([P, SLOTS + HALF], F32, name="work")
+        own = work[:, 0:SLOTS]
+        tanh_b = work[:, SLOTS : SLOTS + HALF]
+        tanh_a = work[:, SLOTS - HALF // 2 : SLOTS + HALF // 2]
+        opp = sb.tile([P, SLOTS], F32, name="opp")
+        diff = sb.tile([P, SLOTS], F32, name="diff")
+        lean = sb.tile([P, SLOTS], F32, name="lean")
+        sa, sbb = slice(0, HALF), slice(HALF, SLOTS)
+        la, lb = slice(0, LIST_COLS // 2), slice(LIST_COLS // 2, LIST_COLS)
+
+        nc.scalar.activation(opp[:, sa], a[:].indirect(l_opp[:, la]), ACT.Copy)
+        nc.scalar.activation(opp[:, sbb], a[:].indirect(l_opp[:, lb]), ACT.Copy)
+        nc.vector.tensor_copy(own[:, sa], a[:].indirect(l_own[:, la]))
+        nc.vector.tensor_tensor(diff[:, sa], a[:].indirect(l_sec[:, la]), opp[:, sa], ALU.subtract)
+        nc.vector.tensor_tensor(diff[:, sbb], a[:].indirect(l_sec[:, lb]), opp[:, sbb], ALU.subtract)
+        nc.scalar.activation(tanh_a, diff[:, sa], ACT.Tanh)
+        nc.scalar.activation(lean[:, sa], tanh_a, ACT.Copy, scale=lam_sb[:])
+        nc.vector.tensor_tensor(f1[:].indirect(l_own[:, la]), own[:, sa], lean[:, sa], ALU.add)
+        nc.scalar.activation(tanh_b, diff[:, sbb], ACT.Tanh)
+        nc.scalar.activation(own[:, sbb], a[:].indirect(l_own[:, lb]), ACT.Copy)
+        nc.scalar.activation(lean[:, sbb], tanh_b, ACT.Copy, scale=lam_sb[:])
+        nc.vector.tensor_tensor(f1[:].indirect(l_own[:, lb]), own[:, sbb], lean[:, sbb], ALU.add)
+        nc.vector.tensor_tensor(f2[:].indirect(l_put[:]), own, lean[:], ALU.add)
+
+        sum_sb = sb.tile([P, T], F32, name="sum_sb")
+        res = sb.tile([P, T], F32, name="res")
+        for b in range(n_pieces):
+            cols = slice(b * PIECE, (b + 1) * PIECE)
+            for lo in range(0, PIECE, P):
+                col = b * PIECE + lo
+                nc.tensor.matmul(
+                    sum_t[b][:, lo : lo + P], f1[:, col : col + P], ident[:],
+                    start=False, stop=(lo == PIECE - P), is_transpose=True,
+                )
+            nc.scalar.copy(sum_sb[:, cols], sum_t[b][:, 0:PIECE])
+        for b in range(n_pieces):
+            cols = slice(b * PIECE, (b + 1) * PIECE)
+            back = ps.tile([P, BANK], F32, name="back%d" % b, tag="bank%d" % (n_pieces + b))
+            for lo in range(0, PIECE, P):
+                col = b * PIECE + lo
+                nc.tensor.transpose(back[:, lo : lo + P], sum_sb[:, col : col + P], ident[:])
+            nc.vector.scalar_tensor_tensor(
+                res[:, cols], f2[:, cols], share_sb[:], back[:, 0:PIECE], ALU.mult, ALU.add
+            )
+            nc.sync.dma_start(out=out[:, cols], in_=res[:, cols])

@@ -18,7 +18,7 @@ ACT = mybir.ActivationFunctionType
 
 P = 128
 PACK = 4
-N_MM = 256
+SCORE_CHUNKS = ((256, True), (256, False), (256, True), (128, False), (128, False))
 HALF = SLOTS // 2
 LIST_COLS = SLOTS // 16
 BANK = 512
@@ -38,17 +38,18 @@ def tile_attend_seconded_lean_twiceput_heads_kernel(
 
         q_raw = sb.tile([P, PACK, Q], F32, name="q_raw")
         nc.sync.dma_start(out=q_raw[:], in_=query.rearrange("(p j) q -> p j q", j=PACK))
-        for quad in range(4):
-            nc.sync.dma_start(
-                out=k_scales[32 * quad : 32 * quad + 4, :].bitcast(I32),
-                in_=keys_scales[0, 4 * quad : 4 * quad + 4, :].bitcast(I32),
-            )
         words_hbm = keys_words[0].rearrange("p n t -> p (n t)").bitcast(I32)
         k_words = []
         for h in range(2):
             tile = sb.tile([P, BANK], U32, name="k_words%d" % h, align_bytes=64)
             nc.sync.dma_start(out=tile[:].bitcast(I32), in_=words_hbm[:, h * BANK : (h + 1) * BANK])
             k_words.append(tile)
+            if h == 0:
+                for quad in range(4):
+                    nc.sync.dma_start(
+                        out=k_scales[32 * quad : 32 * quad + 4, :].bitcast(I32),
+                        in_=keys_scales[0, 4 * quad : 4 * quad + 4, :].bitcast(I32),
+                    )
 
         def load_list(src, name):
             tile = sb.tile([P, LIST_COLS], U16, name=name)
@@ -56,8 +57,8 @@ def tile_attend_seconded_lean_twiceput_heads_kernel(
             return tile
 
         l_opp = load_list(offs3, "l_opp")
-        l_own = load_list(offs, "l_own")
         l_sec = load_list(offs2, "l_sec")
+        l_own = load_list(offs, "l_own")
         lam_sb = sb.tile([P, 1], F32, name="lam_sb")
         nc.sync.dma_start(out=lam_sb[:], in_=lam)
         l_put = load_list(offs4, "l_put")
@@ -74,34 +75,41 @@ def tile_attend_seconded_lean_twiceput_heads_kernel(
         make_identity(nc, ident[:])
 
         q_bf = sb.tile([P, Q, PACK], BF16, name="q_bf", align_bytes=64)
-        nc.vector.tensor_copy(
-            out=q_bf[:].rearrange("p (c i) t -> p c t i", i=4),
-            in_=q_raw[:].rearrange("p t (c i) -> p c t i", i=4),
-        )
         q_codes = sb.tile([P, Q], U32, name="q_codes", align_bytes=64)
         q_scales = sb.tile([P, Q], U8, name="q_scales", align_bytes=64)
-        nc.vector.quantize_mx(
-            out=q_codes[:].bitcast(FP8X4), scales=q_scales[:], in_=q_bf[:].rearrange("p q t -> p (q t)")
-        )
+        q_halves = [slice(0, Q // 2), slice(Q // 2, Q)]
+        for rows in q_halves:
+            nc.vector.tensor_copy(
+                out=q_bf[:, rows, :].rearrange("p (c i) t -> p c t i", i=4),
+                in_=q_raw[:, :, rows].rearrange("p t (c i) -> p c t i", i=4),
+            )
+        for rows in q_halves:
+            nc.vector.quantize_mx(
+                out=q_codes[:, rows].bitcast(FP8X4),
+                scales=q_scales[:, rows],
+                in_=q_bf[:, rows, :].rearrange("p q t -> p (q t)"),
+            )
 
         a = sb.tile([P, T], F32, name="a")
-        for c in range(T // N_MM):
-            cols = slice(c * N_MM, (c + 1) * N_MM)
+        start = 0
+        for c, (width, on_scalar) in enumerate(SCORE_CHUNKS):
+            cols = slice(start, start + width)
             bank = ps.tile([P, BANK], F32, name="scores%d" % c, tag="bank%d" % c)
-            lo = (c * N_MM) % BANK
+            lo = start % BANK
             nc.tensor.matmul_mx(
-                out=bank[:, 0:N_MM],
+                out=bank[:, 0:width],
                 lhsT=q_codes[:].bitcast(FP8X4),
                 lhsT_scale=q_scales[:],
-                rhs=k_words[c * N_MM // BANK][:, lo : lo + N_MM].bitcast(FP8X4),
+                rhs=k_words[start // BANK][:, lo : lo + width].bitcast(FP8X4),
                 rhs_scale=k_scales[:, cols],
                 start=True,
                 stop=True,
             )
-            if c % 2 == 0:
-                nc.scalar.activation(a[:, cols], bank[:, 0:N_MM], ACT.Copy)
+            if on_scalar:
+                nc.scalar.activation(a[:, cols], bank[:, 0:width], ACT.Copy)
             else:
-                nc.vector.tensor_copy(out=a[:, cols], in_=bank[:, 0:N_MM])
+                nc.vector.tensor_copy(out=a[:, cols], in_=bank[:, 0:width])
+            start = start + width
 
         n_pieces = T // PIECE
         sum_t = [ps.tile([P, BANK], F32, name="sum_t%d" % b, tag="bank%d" % b) for b in range(n_pieces)]
@@ -117,21 +125,26 @@ def tile_attend_seconded_lean_twiceput_heads_kernel(
         tanh_b = work[:, SLOTS : SLOTS + HALF]
         tanh_a = work[:, SLOTS - HALF // 2 : SLOTS + HALF // 2]
         opp = sb.tile([P, SLOTS], F32, name="opp")
+        sec_a = sb.tile([P, HALF], F32, name="sec_a")
         diff = sb.tile([P, SLOTS], F32, name="diff")
         lean = sb.tile([P, SLOTS], F32, name="lean")
         sa, sbb = slice(0, HALF), slice(HALF, SLOTS)
         la, lb = slice(0, LIST_COLS // 2), slice(LIST_COLS // 2, LIST_COLS)
 
-        nc.scalar.activation(opp[:, sa], a[:].indirect(l_opp[:, la]), ACT.Copy)
+        nc.vector.tensor_copy(opp[:, sa], a[:].indirect(l_opp[:, la]))
+        nc.scalar.activation(sec_a[:], a[:].indirect(l_sec[:, la]), ACT.Copy)
         nc.scalar.activation(opp[:, sbb], a[:].indirect(l_opp[:, lb]), ACT.Copy)
         nc.vector.tensor_copy(own[:, sa], a[:].indirect(l_own[:, la]))
-        nc.vector.tensor_tensor(diff[:, sa], a[:].indirect(l_sec[:, la]), opp[:, sa], ALU.subtract)
+        nc.vector.tensor_tensor(diff[:, sa], sec_a[:], opp[:, sa], ALU.subtract)
         nc.vector.tensor_tensor(diff[:, sbb], a[:].indirect(l_sec[:, lb]), opp[:, sbb], ALU.subtract)
-        nc.scalar.activation(tanh_a, diff[:, sa], ACT.Tanh)
-        nc.scalar.activation(lean[:, sa], tanh_a, ACT.Copy, scale=lam_sb[:])
+        quarters = [slice(0, HALF // 2), slice(HALF // 2, HALF)]
+        for s in quarters:
+            nc.scalar.activation(tanh_a[:, s], diff[:, s], ACT.Tanh)
+        for s in quarters:
+            nc.scalar.activation(lean[:, s], tanh_a[:, s], ACT.Copy, scale=lam_sb[:])
         nc.vector.tensor_tensor(f1[:].indirect(l_own[:, la]), own[:, sa], lean[:, sa], ALU.add)
-        nc.scalar.activation(tanh_b, diff[:, sbb], ACT.Tanh)
         nc.scalar.activation(own[:, sbb], a[:].indirect(l_own[:, lb]), ACT.Copy)
+        nc.scalar.activation(tanh_b, diff[:, sbb], ACT.Tanh)
         nc.scalar.activation(lean[:, sbb], tanh_b, ACT.Copy, scale=lam_sb[:])
         nc.vector.tensor_tensor(f1[:].indirect(l_own[:, lb]), own[:, sbb], lean[:, sbb], ALU.add)
         nc.vector.tensor_tensor(f2[:].indirect(l_put[:]), own, lean[:], ALU.add)

@@ -38,6 +38,12 @@ def tile_attend_seconded_lean_twiceput_heads_kernel(
 
         q_raw = sb.tile([P, PACK, Q], F32, name="q_raw")
         nc.sync.dma_start(out=q_raw[:], in_=query.rearrange("(p j) q -> p j q", j=PACK))
+        def load_list(src, name):
+            tile = sb.tile([P, LIST_COLS], U16, name=name)
+            nc.sync.dma_start(tile[:], src)
+            return tile
+
+        l_opp = load_list(offs3, "l_opp")
         words_hbm = keys_words[0].rearrange("p n t -> p (n t)").bitcast(I32)
         k_words = []
         for h in range(2):
@@ -51,12 +57,6 @@ def tile_attend_seconded_lean_twiceput_heads_kernel(
                         in_=keys_scales[0, 4 * quad : 4 * quad + 4, :].bitcast(I32),
                     )
 
-        def load_list(src, name):
-            tile = sb.tile([P, LIST_COLS], U16, name=name)
-            nc.sync.dma_start(tile[:], src)
-            return tile
-
-        l_opp = load_list(offs3, "l_opp")
         l_sec = load_list(offs2, "l_sec")
         l_own = load_list(offs, "l_own")
         lam_sb = sb.tile([P, 1], F32, name="lam_sb")
@@ -68,13 +68,11 @@ def tile_attend_seconded_lean_twiceput_heads_kernel(
         nc.sync.dma_start(out=share_sb[:], in_=share2)
 
         f1 = sb.tile([P, T], F32, name="f1")
-        f2 = sb.tile([P, T], F32, name="f2")
         nc.vector.memset(f1[:], 0.0)
-        nc.vector.memset(f2[:], 0.0)
         ident = sb.tile([P, P], F32, name="ident")
         make_identity(nc, ident[:])
 
-        q_bf = sb.tile([P, Q, PACK], BF16, name="q_bf", align_bytes=64)
+        q_bf = sb.tile([P, Q, PACK], BF16, name="q_bf", tag="q_bf_then_f2", align_bytes=64)
         q_codes = sb.tile([P, Q], U32, name="q_codes", align_bytes=64)
         q_scales = sb.tile([P, Q], U8, name="q_scales", align_bytes=64)
         q_halves = [slice(0, Q // 2), slice(Q // 2, Q)]
@@ -89,6 +87,9 @@ def tile_attend_seconded_lean_twiceput_heads_kernel(
                 scales=q_scales[:, rows],
                 in_=q_bf[:, rows, :].rearrange("p q t -> p (q t)"),
             )
+
+        f2 = sb.tile([P, T], F32, name="f2", tag="q_bf_then_f2", align_bytes=64)
+        nc.vector.memset(f2[:], 0.0)
 
         a = sb.tile([P, T], F32, name="a")
         start = 0
@@ -135,9 +136,10 @@ def tile_attend_seconded_lean_twiceput_heads_kernel(
         nc.scalar.activation(sec_a[:], a[:].indirect(l_sec[:, la]), ACT.Copy)
         nc.scalar.activation(opp[:, sbb], a[:].indirect(l_opp[:, lb]), ACT.Copy)
         nc.vector.tensor_copy(own[:, sa], a[:].indirect(l_own[:, la]))
-        nc.vector.tensor_tensor(diff[:, sa], sec_a[:], opp[:, sa], ALU.subtract)
-        nc.vector.tensor_tensor(diff[:, sbb], a[:].indirect(l_sec[:, lb]), opp[:, sbb], ALU.subtract)
         quarters = [slice(0, HALF // 2), slice(HALF // 2, HALF)]
+        for s in quarters:
+            nc.vector.tensor_tensor(diff[:, s], sec_a[:, s], opp[:, s], ALU.subtract)
+        nc.vector.tensor_tensor(diff[:, sbb], a[:].indirect(l_sec[:, lb]), opp[:, sbb], ALU.subtract)
         for s in quarters:
             nc.scalar.activation(tanh_a[:, s], diff[:, s], ACT.Tanh)
         for s in quarters:

from contextlib import ExitStack

import concourse.mybir as mybir
from concourse.masks import make_identity

D, T, SLOTS, Q = 512, 1024, 512, 128
FLOPS = 2 * D * Q * T

F32 = mybir.dt.float32
BF16 = mybir.dt.bfloat16
I32 = mybir.dt.int32
U32 = mybir.dt.uint32
U16 = mybir.dt.uint16
U8 = mybir.dt.uint8
FP8X4 = mybir.dt.float8_e4m3fn_x4
ALU = mybir.AluOpType
ACT = mybir.ActivationFunctionType

P = 128
PACK = 4
SCORE_CHUNKS = ((256, True), (256, False), (256, True), (128, False), (128, False))
HALF = SLOTS // 2
LIST_COLS = SLOTS // 16
BANK = 512
PIECE = 256


def tile_attend_seconded_lean_twiceput_heads_kernel(
    tc, query, keys_words, keys_scales, lam, old, share2, offs, offs2, offs3, offs4, out
):
    nc = tc.nc
    with ExitStack() as ctx:
        sb = ctx.enter_context(tc.tile_pool(name="sb", bufs=1))
        ps = ctx.enter_context(tc.psum_pool(name="ps", bufs=1))

        k_scales = sb.tile([P, T], U8, name="k_scales", align_bytes=64)
        nc.vector.memset(k_scales[:].bitcast(I32), 0)

        q_raw = sb.tile([P, PACK, Q], F32, name="q_raw")
        nc.sync.dma_start(out=q_raw[:], in_=query.rearrange("(p j) q -> p j q", j=PACK))
        def load_list(src, name):
            tile = sb.tile([P, LIST_COLS], U16, name=name)
            nc.sync.dma_start(tile[:], src)
            return tile

        l_opp = load_list(offs3, "l_opp")
        words_hbm = keys_words[0].rearrange("p n t -> p (n t)").bitcast(I32)
        k_words = []
        for h in range(2):
            tile = sb.tile([P, BANK], U32, name="k_words%d" % h, align_bytes=64)
            nc.sync.dma_start(out=tile[:].bitcast(I32), in_=words_hbm[:, h * BANK : (h + 1) * BANK])
            k_words.append(tile)
            if h == 0:
                for quad in range(4):
                    nc.sync.dma_start(
                        out=k_scales[32 * quad : 32 * quad + 4, :].bitcast(I32),
                        in_=keys_scales[0, 4 * quad : 4 * quad + 4, :].bitcast(I32),
                    )

        l_sec = load_list(offs2, "l_sec")
        l_own = load_list(offs, "l_own")
        lam_sb = sb.tile([P, 1], F32, name="lam_sb")
        nc.sync.dma_start(out=lam_sb[:], in_=lam)
        l_put = load_list(offs4, "l_put")
        old_sb = sb.tile([P, T], F32, name="old_sb")
        nc.sync.dma_start(out=old_sb[:], in_=old)
        share_sb = sb.tile([P, 1], F32, name="share_sb")
        nc.sync.dma_start(out=share_sb[:], in_=share2)

        f1 = sb.tile([P, T], F32, name="f1")
        nc.vector.memset(f1[:], 0.0)
        ident = sb.tile([P, P], F32, name="ident")
        make_identity(nc, ident[:])

        q_bf = sb.tile([P, Q, PACK], BF16, name="q_bf", tag="q_bf_then_f2", align_bytes=64)
        q_codes = sb.tile([P, Q], U32, name="q_codes", align_bytes=64)
        q_scales = sb.tile([P, Q], U8, name="q_scales", align_bytes=64)
        q_halves = [slice(0, Q // 2), slice(Q // 2, Q)]
        for rows in q_halves:
            nc.vector.tensor_copy(
                out=q_bf[:, rows, :].rearrange("p (c i) t -> p c t i", i=4),
                in_=q_raw[:, :, rows].rearrange("p t (c i) -> p c t i", i=4),
            )
        for rows in q_halves:
            nc.vector.quantize_mx(
                out=q_codes[:, rows].bitcast(FP8X4),
                scales=q_scales[:, rows],
                in_=q_bf[:, rows, :].rearrange("p q t -> p (q t)"),
            )

        f2 = sb.tile([P, T], F32, name="f2", tag="q_bf_then_f2", align_bytes=64)
        nc.vector.memset(f2[:], 0.0)

        a = sb.tile([P, T], F32, name="a")
        start = 0
        for c, (width, on_scalar) in enumerate(SCORE_CHUNKS):
            cols = slice(start, start + width)
            bank = ps.tile([P, BANK], F32, name="scores%d" % c, tag="bank%d" % c)
            lo = start % BANK
            nc.tensor.matmul_mx(
                out=bank[:, 0:width],
                lhsT=q_codes[:].bitcast(FP8X4),
                lhsT_scale=q_scales[:],
                rhs=k_words[start // BANK][:, lo : lo + width].bitcast(FP8X4),
                rhs_scale=k_scales[:, cols],
                start=True,
                stop=True,
            )
            if on_scalar:
                nc.scalar.activation(a[:, cols], bank[:, 0:width], ACT.Copy)
            else:
                nc.vector.tensor_copy(out=a[:, cols], in_=bank[:, 0:width])
            start = start + width

        n_pieces = T // PIECE
        sum_t = [ps.tile([P, BANK], F32, name="sum_t%d" % b, tag="bank%d" % b) for b in range(n_pieces)]
        for blk in range(T // P):
            b, lo = divmod(blk * P, PIECE)
            nc.tensor.matmul(
                sum_t[b][:, lo : lo + P], old_sb[:, blk * P : (blk + 1) * P], ident[:],
                start=(lo == 0), stop=False, is_transpose=True,
            )

        work = sb.tile([P, SLOTS + HALF], F32, name="work")
        own = work[:, 0:SLOTS]
        tanh_b = work[:, SLOTS : SLOTS + HALF]
        tanh_a = work[:, SLOTS - HALF // 2 : SLOTS + HALF // 2]
        opp = sb.tile([P, SLOTS], F32, name="opp")
        sec_a = sb.tile([P, HALF], F32, name="sec_a")
        diff = sb.tile([P, SLOTS], F32, name="diff")
        lean = sb.tile([P, SLOTS], F32, name="lean")
        sa, sbb = slice(0, HALF), slice(HALF, SLOTS)
        la, lb = slice(0, LIST_COLS // 2), slice(LIST_COLS // 2, LIST_COLS)

        nc.vector.tensor_copy(opp[:, sa], a[:].indirect(l_opp[:, la]))
        nc.scalar.activation(sec_a[:], a[:].indirect(l_sec[:, la]), ACT.Copy)
        nc.scalar.activation(opp[:, sbb], a[:].indirect(l_opp[:, lb]), ACT.Copy)
        nc.vector.tensor_copy(own[:, sa], a[:].indirect(l_own[:, la]))
        quarters = [slice(0, HALF // 2), slice(HALF // 2, HALF)]
        for s in quarters:
            nc.vector.tensor_tensor(diff[:, s], sec_a[:, s], opp[:, s], ALU.subtract)
        nc.vector.tensor_tensor(diff[:, sbb], a[:].indirect(l_sec[:, lb]), opp[:, sbb], ALU.subtract)
        for s in quarters:
            nc.scalar.activation(tanh_a[:, s], diff[:, s], ACT.Tanh)
        for s in quarters:
            nc.scalar.activation(lean[:, s], tanh_a[:, s], ACT.Copy, scale=lam_sb[:])
        nc.vector.tensor_tensor(f1[:].indirect(l_own[:, la]), own[:, sa], lean[:, sa], ALU.add)
        nc.scalar.activation(own[:, sbb], a[:].indirect(l_own[:, lb]), ACT.Copy)
        nc.scalar.activation(tanh_b, diff[:, sbb], ACT.Tanh)
        nc.scalar.activation(lean[:, sbb], tanh_b, ACT.Copy, scale=lam_sb[:])
        nc.vector.tensor_tensor(f1[:].indirect(l_own[:, lb]), own[:, sbb], lean[:, sbb], ALU.add)
        nc.vector.tensor_tensor(f2[:].indirect(l_put[:]), own, lean[:], ALU.add)

        sum_sb = sb.tile([P, T], F32, name="sum_sb")
        res = sb.tile([P, T], F32, name="res")
        for b in range(n_pieces):
            cols = slice(b * PIECE, (b + 1) * PIECE)
            for lo in range(0, PIECE, P):
                col = b * PIECE + lo
                nc.tensor.matmul(
                    sum_t[b][:, lo : lo + P], f1[:, col : col + P], ident[:],
                    start=False, stop=(lo == PIECE - P), is_transpose=True,
                )
            nc.scalar.copy(sum_sb[:, cols], sum_t[b][:, 0:PIECE])
        for b in range(n_pieces):
            cols = slice(b * PIECE, (b + 1) * PIECE)
            back = ps.tile([P, BANK], F32, name="back%d" % b, tag="bank%d" % (n_pieces + b))
            for lo in range(0, PIECE, P):
                col = b * PIECE + lo
                nc.tensor.transpose(back[:, lo : lo + P], sum_sb[:, col : col + P], ident[:])
            nc.vector.scalar_tensor_tensor(
                res[:, cols], f2[:, cols], share_sb[:], back[:, 0:PIECE], ALU.mult, ALU.add
            )
            nc.sync.dma_start(out=out[:, cols], in_=res[:, cols])
